import numpy as np
import ml_dtypes


def mxq(x, axis, fmt="e4m3"):
    dtype, down = {"e4m3": (ml_dtypes.float8_e4m3fn, 7), "e5m2": (ml_dtypes.float8_e5m2, 14)}[fmt]
    v = np.moveaxis(np.asarray(x, np.float32).astype(ml_dtypes.bfloat16).astype(np.float64), axis, -1)
    blocks = v.reshape(v.shape[:-1] + (-1, 32))
    amax = np.abs(blocks).max(-1, keepdims=True)
    byte = np.maximum(np.where(amax > 0, np.frexp(amax)[1] - 1 + 127, 0) - down, 1)
    scale = np.exp2(byte - 127.0)
    codes = (blocks / scale).astype(np.float32).astype(dtype).astype(np.float64)
    return np.moveaxis((codes * scale).reshape(v.shape), -1, axis)


WIDE = False


def mx_kscale(k):
    if not WIDE:
        return np.ones(k)
    levels = np.array([10, -10, 5, -5, 0])
    if k % 512:
        return np.exp2(np.random.permutation(np.resize(levels, k // 32))).repeat(32)
    a = np.empty((k // 512, 16))
    for p in range(k // 512):
        a[p, :8] = np.random.permutation(np.resize(levels, 8))
        for g in range(8):
            far = levels[np.abs(levels - a[p, g]) >= 10]
            a[p, g + 8] = far[np.random.randint(len(far))]
    return np.exp2(a.ravel()).repeat(32)


def f64(x):
    return np.asarray(x).astype(np.float64)


def striped8(idx):
    return np.concatenate([x.reshape(-1, 16).T for x in idx]).astype(np.uint16)


def runs(offs, k):
    lists = np.stack([offs[16 * r : 16 * r + 16].T.reshape(-1) for r in range(8)]).astype(np.int64)
    return lists[np.arange(k) % 512 // 64]


def pack_weight(w):
    k, n = w.shape
    w = f64(np.asarray(w, np.float32).astype(ml_dtypes.bfloat16)).reshape(k // 32, 32, n)
    amax = np.abs(w).max(1)
    byte = np.clip(np.where(amax > 0, np.frexp(amax)[1] - 1 + 127 - 7, 1), 1, 254)
    scaled = (w * np.exp2(127.0 - byte)[:, None, :]).reshape(k, n).astype(np.float32)
    words = np.ascontiguousarray(scaled.reshape(k // 512, 128, 4, n).transpose(0, 1, 3, 2)).astype(ml_dtypes.float8_e4m3fn).view(np.uint8)
    return words, np.ascontiguousarray(byte.astype(np.uint8).reshape(k // 512, 16, n))


def unpack_weight(words, scales):
    g, p, n, _ = words.shape
    vals = np.ascontiguousarray(words).view(ml_dtypes.float8_e4m3fn).astype(np.float64) * np.repeat(np.exp2(scales.astype(np.float64) - 127.0), 8, axis=1)[..., None]
    return vals.transpose(0, 1, 3, 2).reshape(g * 512, n)


def sigmoid(v):
    return 1.0 / (1.0 + np.exp(-np.maximum(v, -700.0)))


K, T, S, N = 512, 2048, 512, 512


def setup_inputs():
    n = np.random.standard_normal
    s = mx_kscale(K)[:, None]
    packed_xT = pack_weight(n((K, T)) * s)
    return {
        "x_words": packed_xT[0],
        "x_scales": packed_xT[1],
        "w1": (n((K, N)) / np.sqrt(3 * K) / s).astype(np.float32),
        "w2": (n((K, N)) / np.sqrt(3 * K) / s).astype(np.float32),
        "w3": (n((K, N)) / np.sqrt(3 * K) / s).astype(np.float32),
        "w4": (n((K, N)) / np.sqrt(3 * K) / s).astype(np.float32),
        "w5": (n((K, N)) / np.sqrt(3 * K) / s).astype(np.float32),
        "w6": (n((K, N)) / np.sqrt(3 * K) / s).astype(np.float32),
        "offs": striped8(np.stack([np.random.permutation(T)[:S] for _ in range(8)])),
        "tap1": striped8(np.stack([np.random.permutation(T)[:S] for _ in range(8)])),
        "tap2": striped8(np.stack([np.random.permutation(T)[:S] for _ in range(8)])),
    }


def reference(x_words, x_scales, w1, w2, w3, w4, w5, w6, offs, tap1, tap2):
    xq = unpack_weight(x_words, x_scales)[np.arange(K)[:, None], runs(offs, K)]
    x_tap1 = unpack_weight(x_words, x_scales)[np.arange(K)[:, None], runs(tap1, K)]
    x_tap2 = unpack_weight(x_words, x_scales)[np.arange(K)[:, None], runs(tap2, K)]
    o = mxq(f64(w1), 0, "e4m3").T @ xq + mxq(f64(w2), 0, "e4m3").T @ x_tap1 + mxq(f64(w3), 0, "e4m3").T @ x_tap2
    s = sigmoid(mxq(f64(w4), 0, "e4m3").T @ xq + mxq(f64(w5), 0, "e4m3").T @ x_tap1 + mxq(f64(w6), 0, "e4m3").T @ x_tap2)
    return o * s

@@ -1,0 +1,143 @@
+from contextlib import ExitStack
+
+import concourse.mybir as mybir
+
+F32 = mybir.dt.float32
+BF16 = mybir.dt.bfloat16
+I32 = mybir.dt.int32
+U32 = mybir.dt.uint32
+U16 = mybir.dt.uint16
+U8 = mybir.dt.uint8
+FP8X4 = mybir.dt.float8_e4m3fn_x4
+
+P = 128
+PACK = 4
+K, T, S, N = 512, 2048, 512, 512
+TAPS = 3
+HALF = 256
+BLOCK = 128
+EARLY = 5
+FLOPS = 2 * 2 * TAPS * K * N * S
+
+
+def tile_picked_gdconv_none_p_kernel(tc, x_words, x_scales, w1, w2, w3, w4, w5, w6, offs, tap1, tap2, out):
+    nc = tc.nc
+    with ExitStack() as ctx:
+        keep = ctx.enter_context(tc.tile_pool(name="keep", bufs=1))
+        psum = ctx.enter_context(tc.psum_pool(name="psum", bufs=1))
+
+        lists = []
+        for t, src in enumerate((offs, tap1, tap2)):
+            tl = keep.tile([P, S // 16], U16, name=f"list{t}")
+            nc.sync.dma_start(tl[:], src)
+            lists.append(tl)
+
+        scale_table = keep.tile([P, T], U8, name="scale_table", tag="shared", align_bytes=64)
+        nc.vector.memset(scale_table[:].bitcast(I32), 0)
+        warm = keep.tile([P, 16], F32, name="warm")
+        nc.gpsimd.memset(warm[:, 0:1], 0.0)
+        nc.scalar.activation(warm[:, 8:9], warm[:, 0:1], mybir.ActivationFunctionType.Sigmoid)
+        rows = x_scales[0].bitcast(I32)
+        x_plane = keep.tile([P, TAPS * S], U8, name="x_plane", align_bytes=64)
+        nc.vector.memset(x_plane[:].bitcast(I32), 0)
+
+        weights = {"g": (w4, w5, w6), "o": (w1, w2, w3)}
+        raw = {}
+
+        def load(unit, tl):
+            kind, t, h = unit
+            nc.sync.dma_start(tl, weights[kind][t].rearrange("(p j) m -> p j m", j=PACK)[:, :, h * HALF : (h + 1) * HALF])
+            raw[unit] = tl
+
+        units = [(kind, t, h) for h in range(2) for kind in ("g", "o") for t in range(TAPS)]
+        early = [keep.tile([P, PACK, HALF], F32, name=f"early{u}") for u in range(EARLY)]
+        load(units[0], early[0][:])
+        for i in range(2):
+            nc.sync.dma_start(scale_table[i:P:16, :].bitcast(I32), rows[i:16:2, :])
+        word_table = keep.tile([P, T], I32, name="word_table", align_bytes=64)
+        nc.sync.dma_start(word_table[:], x_words[0].rearrange("p n t -> p (n t)").bitcast(I32))
+        for u in range(1, EARLY):
+            load(units[u], early[u][:])
+
+        picked_scales = keep.tile([P, TAPS * S], U8, name="picked_scales", align_bytes=64)
+        for t in range(TAPS):
+            nc.vector.tensor_copy(picked_scales[:, t * S : (t + 1) * S], scale_table[:].indirect(lists[t][:]))
+        for i in range(4):
+            nc.sync.dma_start(x_plane[i:P:32, :].bitcast(I32), picked_scales[16 * (i // 2) + i % 2 : P : 32, :].bitcast(I32))
+        late = keep.tile([P, (len(units) - EARLY) * PACK * HALF], F32, name="late", tag="shared", align_bytes=64)
+        for u in range(EARLY, len(units)):
+            at = (u - EARLY) * PACK * HALF
+            load(units[u], late[:, at : at + PACK * HALF].rearrange("p (j m) -> p j m", j=PACK))
+
+        codes = {}
+
+        def cast(engine, kind, t, h, lo, width):
+            grouped = keep.tile([P, width, PACK], BF16, name=f"bf_{kind}{t}{h}{lo}", tag=f"bf_{kind}{t}{h}{lo}", align_bytes=64)
+            dst = grouped[:].rearrange("p (c i) j -> p c j i", i=4)
+            src = raw[kind, t, h][:, :, lo : lo + width].rearrange("p j (c i) -> p c j i", i=4)
+            if engine == "s":
+                nc.scalar.copy(dst, src)
+            else:
+                nc.vector.tensor_copy(dst, src)
+            return grouped
+
+        def quantise(grouped, kind, t, h, lo, width):
+            words = keep.tile([P, width], U32, name=f"q_{kind}{t}{h}{lo}", align_bytes=64)
+            plane = keep.tile([P, width], U8, name=f"s_{kind}{t}{h}{lo}", align_bytes=64)
+            nc.vector.quantize_mx(out=words[:].bitcast(FP8X4), scales=plane[:], in_=grouped[:].rearrange("p c j -> p (c j)"))
+            for b in range(width // BLOCK):
+                codes[kind, t, 2 * h + lo // BLOCK + b] = (words[:, b * BLOCK : (b + 1) * BLOCK], plane[:, b * BLOCK : (b + 1) * BLOCK])
+
+        picked = {}
+
+        def pick(t, tag):
+            picked[t] = keep.tile([P, S], U32, name=f"picked{t}", tag=tag, align_bytes=64)
+            nc.vector.tensor_copy(picked[t][:], word_table[:].bitcast(U32).indirect(lists[t][:]))
+
+        pick(0, "picked0")
+        pick(1, "picked1")
+
+        acc = {}
+        for kind in ("g", "o"):
+            for b in range(4):
+                acc[kind, b] = psum.tile([P, S], F32, name=f"acc_{kind}{b}")
+
+        def product(kind, t, b):
+            words, plane = codes[kind, t, b]
+            nc.tensor.matmul_mx(out=acc[kind, b][:], lhsT=words.bitcast(FP8X4), lhsT_scale=plane,
+                                rhs=picked[t][:].bitcast(FP8X4), rhs_scale=x_plane[:, t * S : (t + 1) * S],
+                                start=(t == 0), stop=(t == TAPS - 1))
+
+        gate = {}
+
+        def sigmoid(b):
+            if b % 2 == 0:
+                pair = keep.tile([P, 2 * S], F32, name=f"gate{b}", tag=("bf_o100" if b == 0 else "gate_b"), align_bytes=64)
+                gate[b], gate[b + 1] = pair[:, :S], pair[:, S:]
+            nc.scalar.activation(gate[b], acc["g", b][:], mybir.ActivationFunctionType.Sigmoid)
+
+        def finish(b):
+            res = keep.tile([P, S], F32, name=f"res{b}")
+            nc.vector.tensor_tensor(res[:], acc["o", b][:], gate[b], mybir.AluOpType.mult)
+            nc.sync.dma_start(out[b * BLOCK : (b + 1) * BLOCK, :], res[:])
+
+        on_vector = {("g", 0, 1), ("o", 1, 1)}
+        for h in range(2):
+            for kind in ("g", "o"):
+                for t in range(TAPS):
+                    if (kind, t, h) == ("g", 2, 0):
+                        pick(2, "bf_g100")
+                    if (kind, t, h) == ("o", 2, 1):
+                        parts = [(cast(e, kind, t, h, lo, BLOCK), lo) for e, lo in (("v", 0), ("s", BLOCK))]
+                        for grouped, lo in parts:
+                            quantise(grouped, kind, t, h, lo, BLOCK)
+                    else:
+                        grouped = cast("v" if (kind, t, h) in on_vector else "s", kind, t, h, 0, HALF)
+                        quantise(grouped, kind, t, h, 0, HALF)
+                    for b in (2 * h, 2 * h + 1):
+                        product(kind, t, b)
+                    if (kind, t) == ("o", 1 - h):
+                        for b in (2 * h, 2 * h + 1):
+                            sigmoid(b)
+            for b in (2 * h, 2 * h + 1):
+                finish(b)

@@ -16,7 +16,7 @@ K, T, S, N = 512, 2048, 512, 512
 TAPS = 3
 HALF = 256
 BLOCK = 128
-EARLY = 5
+HEAD = 512
 FLOPS = 2 * 2 * TAPS * K * N * S
 
 
@@ -44,49 +44,51 @@ def tile_picked_gdconv_none_p_kernel(tc, x_words, x_scales, w1, w2, w3, w4, w5, 
         weights = {"g": (w4, w5, w6), "o": (w1, w2, w3)}
         raw = {}
 
-        def load(unit, tl):
-            kind, t, h = unit
-            nc.sync.dma_start(tl, weights[kind][t].rearrange("(p j) m -> p j m", j=PACK)[:, :, h * HALF : (h + 1) * HALF])
-            raw[unit] = tl
+        def load(kind, t, tl, lo, width):
+            nc.sync.dma_start(tl, weights[kind][t].rearrange("(p j) m -> p j m", j=PACK)[:, :, lo : lo + width])
+            for b in range(width // BLOCK):
+                raw[kind, t, lo + b * BLOCK] = (tl, b * BLOCK)
 
-        units = [(kind, t, h) for h in range(2) for kind in ("g", "o") for t in range(TAPS)]
-        early = [keep.tile([P, PACK, HALF], F32, name=f"early{u}") for u in range(EARLY)]
-        load(units[0], early[0][:])
+        word_table = keep.tile([P, T], I32, name="word_table", align_bytes=64)
+        words_in = x_words[0].rearrange("p n t -> p (n t)").bitcast(I32)
+        nc.sync.dma_start(word_table[:, :HEAD], words_in[:, :HEAD])
         for i in range(2):
             nc.sync.dma_start(scale_table[i:P:16, :].bitcast(I32), rows[i:16:2, :])
-        word_table = keep.tile([P, T], I32, name="word_table", align_bytes=64)
-        nc.sync.dma_start(word_table[:], x_words[0].rearrange("p n t -> p (n t)").bitcast(I32))
-        for u in range(1, EARLY):
-            load(units[u], early[u][:])
+        early = [keep.tile([P, PACK, N], F32, name=f"early{u}") for u in range(2)]
+        load("g", 0, early[0][:], 0, N)
+        nc.sync.dma_start(word_table[:, HEAD:], words_in[:, HEAD:])
+        load("g", 1, early[1][:], 0, N)
 
         picked_scales = keep.tile([P, TAPS * S], U8, name="picked_scales", align_bytes=64)
         for t in range(TAPS):
             nc.vector.tensor_copy(picked_scales[:, t * S : (t + 1) * S], scale_table[:].indirect(lists[t][:]))
         for i in range(4):
             nc.sync.dma_start(x_plane[i:P:32, :].bitcast(I32), picked_scales[16 * (i // 2) + i % 2 : P : 32, :].bitcast(I32))
-        late = keep.tile([P, (len(units) - EARLY) * PACK * HALF], F32, name="late", tag="shared", align_bytes=64)
-        for u in range(EARLY, len(units)):
-            at = (u - EARLY) * PACK * HALF
-            load(units[u], late[:, at : at + PACK * HALF].rearrange("p (j m) -> p j m", j=PACK))
+        late = keep.tile([P, (TAPS + 1) * PACK * N], F32, name="late", tag="shared", align_bytes=64)
+        at = 0
+        for kind, t, lo, width in (("g", 2, 0, N), ("o", 0, 0, N), ("o", 1, 0, N), ("o", 2, 0, HALF), ("o", 2, HALF, HALF)):
+            load(kind, t, late[:, at : at + PACK * width].rearrange("p (j m) -> p j m", j=PACK), lo, width)
+            at = at + PACK * width
 
         codes = {}
 
-        def cast(engine, kind, t, h, lo, width):
-            grouped = keep.tile([P, width, PACK], BF16, name=f"bf_{kind}{t}{h}{lo}", tag=f"bf_{kind}{t}{h}{lo}", align_bytes=64)
+        def cast(engine, kind, t, lo, width):
+            grouped = keep.tile([P, width, PACK], BF16, name=f"bf_{kind}{t}{lo}", tag=f"bf_{kind}{t}{lo}", align_bytes=64)
             dst = grouped[:].rearrange("p (c i) j -> p c j i", i=4)
-            src = raw[kind, t, h][:, :, lo : lo + width].rearrange("p j (c i) -> p c j i", i=4)
+            tl, at = raw[kind, t, lo]
+            src = tl[:, :, at : at + width].rearrange("p j (c i) -> p c j i", i=4)
             if engine == "s":
                 nc.scalar.copy(dst, src)
             else:
                 nc.vector.tensor_copy(dst, src)
             return grouped
 
-        def quantise(grouped, kind, t, h, lo, width):
-            words = keep.tile([P, width], U32, name=f"q_{kind}{t}{h}{lo}", align_bytes=64)
-            plane = keep.tile([P, width], U8, name=f"s_{kind}{t}{h}{lo}", align_bytes=64)
+        def quantise(grouped, kind, t, lo, width):
+            words = keep.tile([P, width], U32, name=f"q_{kind}{t}{lo}", align_bytes=64)
+            plane = keep.tile([P, width], U8, name=f"s_{kind}{t}{lo}", align_bytes=64)
             nc.vector.quantize_mx(out=words[:].bitcast(FP8X4), scales=plane[:], in_=grouped[:].rearrange("p c j -> p (c j)"))
             for b in range(width // BLOCK):
-                codes[kind, t, 2 * h + lo // BLOCK + b] = (words[:, b * BLOCK : (b + 1) * BLOCK], plane[:, b * BLOCK : (b + 1) * BLOCK])
+                codes[kind, t, lo // BLOCK + b] = (words[:, b * BLOCK : (b + 1) * BLOCK], plane[:, b * BLOCK : (b + 1) * BLOCK])
 
         picked = {}
 
@@ -111,33 +113,29 @@ def tile_picked_gdconv_none_p_kernel(tc, x_words, x_scales, w1, w2, w3, w4, w5, 
         gate = {}
 
         def sigmoid(b):
-            if b % 2 == 0:
-                pair = keep.tile([P, 2 * S], F32, name=f"gate{b}", tag=("bf_o100" if b == 0 else "gate_b"), align_bytes=64)
-                gate[b], gate[b + 1] = pair[:, :S], pair[:, S:]
-            nc.scalar.activation(gate[b], acc["g", b][:], mybir.ActivationFunctionType.Sigmoid)
+            gate[b] = keep.tile([P, S], F32, name=f"gate{b}")
+            nc.scalar.activation(gate[b][:], acc["g", b][:], mybir.ActivationFunctionType.Sigmoid)
 
         def finish(b):
             res = keep.tile([P, S], F32, name=f"res{b}")
-            nc.vector.tensor_tensor(res[:], acc["o", b][:], gate[b], mybir.AluOpType.mult)
+            nc.vector.tensor_tensor(res[:], acc["o", b][:], gate[b][:], mybir.AluOpType.mult)
             nc.sync.dma_start(out[b * BLOCK : (b + 1) * BLOCK, :], res[:])
 
-        on_vector = {("g", 0, 1), ("o", 1, 1)}
-        for h in range(2):
-            for kind in ("g", "o"):
-                for t in range(TAPS):
-                    if (kind, t, h) == ("g", 2, 0):
-                        pick(2, "bf_g100")
-                    if (kind, t, h) == ("o", 2, 1):
-                        parts = [(cast(e, kind, t, h, lo, BLOCK), lo) for e, lo in (("v", 0), ("s", BLOCK))]
-                        for grouped, lo in parts:
-                            quantise(grouped, kind, t, h, lo, BLOCK)
-                    else:
-                        grouped = cast("v" if (kind, t, h) in on_vector else "s", kind, t, h, 0, HALF)
-                        quantise(grouped, kind, t, h, 0, HALF)
+        engines = {("g", 0): "ss", ("g", 1): "ss", ("g", 2): "ss", ("o", 0): "sv", ("o", 1): "vs", ("o", 2): ("v", "ss")}
+        for kind in ("g", "o"):
+            for t in range(TAPS):
+                if (kind, t) == ("g", 2):
+                    pick(2, "picked2")
+                for h in range(2):
+                    who = engines[kind, t][h]
+                    width = HALF // len(who)
+                    parts = [(cast(e, kind, t, h * HALF + n * width, width), h * HALF + n * width) for n, e in enumerate(who)]
+                    for grouped, lo in parts:
+                        quantise(grouped, kind, t, lo, width)
                     for b in (2 * h, 2 * h + 1):
                         product(kind, t, b)
-                    if (kind, t) == ("o", 1 - h):
-                        for b in (2 * h, 2 * h + 1):
-                            sigmoid(b)
-            for b in (2 * h, 2 * h + 1):
-                finish(b)
+                if (kind, t) == ("o", 0):
+                    for b in range(4):
+                        sigmoid(b)
+        for b in range(4):
+            finish(b)

@@ -121,7 +121,7 @@ def tile_picked_gdconv_none_p_kernel(tc, x_words, x_scales, w1, w2, w3, w4, w5, 
             nc.vector.tensor_tensor(res[:], acc["o", b][:], gate[b][:], mybir.AluOpType.mult)
             nc.sync.dma_start(out[b * BLOCK : (b + 1) * BLOCK, :], res[:])
 
-        engines = {("g", 0): "ss", ("g", 1): "ss", ("g", 2): "ss", ("o", 0): "sv", ("o", 1): "vs", ("o", 2): ("v", "ss")}
+        engines = {("g", 0): "ss", ("g", 1): "ss", ("g", 2): ("ss", "v"), ("o", 0): "vv", ("o", 1): "sv", ("o", 2): ("sv", "sv")}
         for kind in ("g", "o"):
             for t in range(TAPS):
                 if (kind, t) == ("g", 2):
@@ -134,7 +134,7 @@ def tile_picked_gdconv_none_p_kernel(tc, x_words, x_scales, w1, w2, w3, w4, w5, 
                         quantise(grouped, kind, t, lo, width)
                     for b in (2 * h, 2 * h + 1):
                         product(kind, t, b)
-                if (kind, t) == ("o", 0):
+                if (kind, t) == ("g", 2):
                     for b in range(4):
                         sigmoid(b)
         for b in range(4):

@@ -16,7 +16,6 @@ K, T, S, N = 512, 2048, 512, 512
 TAPS = 3
 HALF = 256
 BLOCK = 128
-HEAD = 512
 FLOPS = 2 * 2 * TAPS * K * N * S
 
 
@@ -26,20 +25,19 @@ def tile_picked_gdconv_none_p_kernel(tc, x_words, x_scales, w1, w2, w3, w4, w5, 
         keep = ctx.enter_context(tc.tile_pool(name="keep", bufs=1))
         psum = ctx.enter_context(tc.psum_pool(name="psum", bufs=1))
 
+        scale_table = keep.tile([P, T], U8, name="scale_table", tag="shared", align_bytes=64)
+        nc.gpsimd.memset(scale_table[:].bitcast(I32), 0)
         lists = []
         for t, src in enumerate((offs, tap1, tap2)):
             tl = keep.tile([P, S // 16], U16, name=f"list{t}")
             nc.sync.dma_start(tl[:], src)
             lists.append(tl)
-
-        scale_table = keep.tile([P, T], U8, name="scale_table", tag="shared", align_bytes=64)
-        nc.vector.memset(scale_table[:].bitcast(I32), 0)
+        nc.sync.dma_start(scale_table[0:P:8, :].bitcast(I32), x_scales[0].bitcast(I32))
         warm = keep.tile([P, 16], F32, name="warm")
         nc.gpsimd.memset(warm[:, 0:1], 0.0)
         nc.scalar.activation(warm[:, 8:9], warm[:, 0:1], mybir.ActivationFunctionType.Sigmoid)
-        rows = x_scales[0].bitcast(I32)
         x_plane = keep.tile([P, TAPS * S], U8, name="x_plane", align_bytes=64)
-        nc.vector.memset(x_plane[:].bitcast(I32), 0)
+        nc.gpsimd.memset(x_plane[:].bitcast(I32), 0)
 
         weights = {"g": (w4, w5, w6), "o": (w1, w2, w3)}
         raw = {}
@@ -51,44 +49,48 @@ def tile_picked_gdconv_none_p_kernel(tc, x_words, x_scales, w1, w2, w3, w4, w5, 
 
         word_table = keep.tile([P, T], I32, name="word_table", align_bytes=64)
         words_in = x_words[0].rearrange("p n t -> p (n t)").bitcast(I32)
-        nc.sync.dma_start(word_table[:, :HEAD], words_in[:, :HEAD])
-        for i in range(2):
-            nc.sync.dma_start(scale_table[i:P:16, :].bitcast(I32), rows[i:16:2, :])
         early = [keep.tile([P, PACK, N], F32, name=f"early{u}") for u in range(2)]
+        nc.sync.dma_start(word_table[:], words_in)
         load("g", 0, early[0][:], 0, N)
-        nc.sync.dma_start(word_table[:, HEAD:], words_in[:, HEAD:])
         load("g", 1, early[1][:], 0, N)
 
         picked_scales = keep.tile([P, TAPS * S], U8, name="picked_scales", align_bytes=64)
         for t in range(TAPS):
             nc.vector.tensor_copy(picked_scales[:, t * S : (t + 1) * S], scale_table[:].indirect(lists[t][:]))
         for i in range(4):
-            nc.sync.dma_start(x_plane[i:P:32, :].bitcast(I32), picked_scales[16 * (i // 2) + i % 2 : P : 32, :].bitcast(I32))
+            nc.sync.dma_start(x_plane[i:P:32, :].bitcast(I32), picked_scales[8 * i : P : 32, :].bitcast(I32))
         late = keep.tile([P, (TAPS + 1) * PACK * N], F32, name="late", tag="shared", align_bytes=64)
         at = 0
-        for kind, t, lo, width in (("g", 2, 0, N), ("o", 0, 0, N), ("o", 1, 0, N), ("o", 2, 0, HALF), ("o", 2, HALF, HALF)):
+        for kind, t, lo, width in (("g", 2, 0, N), ("o", 0, 0, N), ("o", 1, 0, N), ("o", 2, 0, HALF), ("o", 2, HALF, BLOCK), ("o", 2, 3 * BLOCK, BLOCK)):
             load(kind, t, late[:, at : at + PACK * width].rearrange("p (j m) -> p j m", j=PACK), lo, width)
             at = at + PACK * width
 
         codes = {}
+        rounded = {}
 
-        def cast(engine, kind, t, lo, width):
-            grouped = keep.tile([P, width, PACK], BF16, name=f"bf_{kind}{t}{lo}", tag=f"bf_{kind}{t}{lo}", align_bytes=64)
-            dst = grouped[:].rearrange("p (c i) j -> p c j i", i=4)
-            tl, at = raw[kind, t, lo]
-            src = tl[:, :, at : at + width].rearrange("p j (c i) -> p c j i", i=4)
+        def stage(tag, pieces):
+            tl = keep.tile([P, len(pieces) * BLOCK, PACK], BF16, name="bf_%s%d%d" % pieces[0], tag=tag, align_bytes=64)
+            for n, piece in enumerate(pieces):
+                rounded[piece] = (tl, n * BLOCK)
+
+        def cast(engine, kind, t, first, count):
+            tl, at = rounded[kind, t, first]
+            dst = tl[:, at : at + count * BLOCK, :].rearrange("p (c i) j -> p c j i", i=4)
+            tl, at = raw[kind, t, first * BLOCK]
+            src = tl[:, :, at : at + count * BLOCK].rearrange("p j (c i) -> p c j i", i=4)
             if engine == "s":
                 nc.scalar.copy(dst, src)
             else:
                 nc.vector.tensor_copy(dst, src)
-            return grouped
 
-        def quantise(grouped, kind, t, lo, width):
-            words = keep.tile([P, width], U32, name=f"q_{kind}{t}{lo}", align_bytes=64)
-            plane = keep.tile([P, width], U8, name=f"s_{kind}{t}{lo}", align_bytes=64)
-            nc.vector.quantize_mx(out=words[:].bitcast(FP8X4), scales=plane[:], in_=grouped[:].rearrange("p c j -> p (c j)"))
-            for b in range(width // BLOCK):
-                codes[kind, t, lo // BLOCK + b] = (words[:, b * BLOCK : (b + 1) * BLOCK], plane[:, b * BLOCK : (b + 1) * BLOCK])
+        def quantise(kind, t, first, count, words_tag="", plane_tag=""):
+            width = count * BLOCK
+            words = keep.tile([P, width], U32, name=f"q_{kind}{t}{first}", tag=words_tag or f"q_{kind}{t}{first}", align_bytes=64)
+            plane = keep.tile([P, width], U8, name=f"s_{kind}{t}{first}", tag=plane_tag or f"s_{kind}{t}{first}", align_bytes=64)
+            tl, at = rounded[kind, t, first]
+            nc.vector.quantize_mx(out=words[:].bitcast(FP8X4), scales=plane[:], in_=tl[:, at : at + width, :].rearrange("p c j -> p (c j)"))
+            for b in range(count):
+                codes[kind, t, first + b] = (words[:, b * BLOCK : (b + 1) * BLOCK], plane[:, b * BLOCK : (b + 1) * BLOCK])
 
         picked = {}
 
@@ -113,7 +115,7 @@ def tile_picked_gdconv_none_p_kernel(tc, x_words, x_scales, w1, w2, w3, w4, w5, 
         gate = {}
 
         def sigmoid(b):
-            gate[b] = keep.tile([P, S], F32, name=f"gate{b}")
+            gate[b] = keep.tile([P, S], F32, name=f"gate{b}", tag=f"gate{b}", align_bytes=64)
             nc.scalar.activation(gate[b][:], acc["g", b][:], mybir.ActivationFunctionType.Sigmoid)
 
         def finish(b):
@@ -121,21 +123,39 @@ def tile_picked_gdconv_none_p_kernel(tc, x_words, x_scales, w1, w2, w3, w4, w5, 
             nc.vector.tensor_tensor(res[:], acc["o", b][:], gate[b][:], mybir.AluOpType.mult)
             nc.sync.dma_start(out[b * BLOCK : (b + 1) * BLOCK, :], res[:])
 
-        engines = {("g", 0): "ss", ("g", 1): "ss", ("g", 2): ("ss", "v"), ("o", 0): "vv", ("o", 1): "sv", ("o", 2): ("sv", "sv")}
-        for kind in ("g", "o"):
-            for t in range(TAPS):
-                if (kind, t) == ("g", 2):
-                    pick(2, "picked2")
-                for h in range(2):
-                    who = engines[kind, t][h]
-                    width = HALF // len(who)
-                    parts = [(cast(e, kind, t, h * HALF + n * width, width), h * HALF + n * width) for n, e in enumerate(who)]
-                    for grouped, lo in parts:
-                        quantise(grouped, kind, t, lo, width)
-                    for b in (2 * h, 2 * h + 1):
-                        product(kind, t, b)
-                if (kind, t) == ("g", 2):
-                    for b in range(4):
-                        sigmoid(b)
+        def step(engine, kind, t, first, count, **tags):
+            cast(engine, kind, t, first, count)
+            quantise(kind, t, first, count, **tags)
+            for b in range(first, first + count):
+                product(kind, t, b)
+
+        for t in range(2):
+            if t == 1:
+                pick(2, "bf02")
+            for first in (0, 2):
+                stage("vector_stage" if (t, first) == (1, 2) else f"bf{t}{first}", [("g", t, first), ("g", t, first + 1)])
+                step("s", "g", t, first, 2)
+        stage("vector_stage", [("g", 2, 0), ("g", 2, 1)])
+        stage("bf22", [("g", 2, 2), ("g", 2, 3)])
+        for b in range(3):
+            step("vvs"[b], "g", 2, b, 1, words_tag="tail_c" if b == 2 else "", plane_tag="last" if b == 2 else "")
+            sigmoid(b)
+        step("s", "g", 2, 3, 1, words_tag="tail_a", plane_tag="tail_b")
+        sigmoid(3)
+        stage("vector_stage", [("o", 0, b) for b in range(4)])
+        step("v", "o", 0, 0, 2)
+        step("v", "o", 0, 2, 2)
+        stage("vector_stage", [("o", 1, 0), ("o", 1, 1)])
+        stage("tail_b", [("o", 1, 2)])
+        stage("tail_a", [("o", 1, 3), ("o", 2, 1)])
+        stage("tail_c", [("o", 2, 2)])
+        for b in range(4):
+            step("vvss"[b], "o", 1, b, 1)
+        stage("tail_b", [("o", 2, 0)])
+        step("v", "o", 2, 0, 1)
+        step("s", "o", 2, 1, 1)
+        step("s", "o", 2, 2, 1)
+        stage("last", [("o", 2, 3)])
+        step("s", "o", 2, 3, 1)
         for b in range(4):
             finish(b)

@@ -16,6 +16,7 @@ K, T, S, N = 512, 2048, 512, 512
 TAPS = 3
 HALF = 256
 BLOCK = 128
+HEAD = 512
 FLOPS = 2 * 2 * TAPS * K * N * S
 
 
@@ -27,6 +28,9 @@ def tile_picked_gdconv_none_p_kernel(tc, x_words, x_scales, w1, w2, w3, w4, w5, 
 
         scale_table = keep.tile([P, T], U8, name="scale_table", tag="shared", align_bytes=64)
         nc.gpsimd.memset(scale_table[:].bitcast(I32), 0)
+        word_table = keep.tile([P, T], I32, name="word_table", align_bytes=64)
+        words_in = x_words[0].rearrange("p n t -> p (n t)").bitcast(I32)
+        nc.sync.dma_start(word_table[:, :HEAD], words_in[:, :HEAD])
         lists = []
         for t, src in enumerate((offs, tap1, tap2)):
             tl = keep.tile([P, S // 16], U16, name=f"list{t}")
@@ -47,10 +51,8 @@ def tile_picked_gdconv_none_p_kernel(tc, x_words, x_scales, w1, w2, w3, w4, w5, 
             for b in range(width // BLOCK):
                 raw[kind, t, lo + b * BLOCK] = (tl, b * BLOCK)
 
-        word_table = keep.tile([P, T], I32, name="word_table", align_bytes=64)
-        words_in = x_words[0].rearrange("p n t -> p (n t)").bitcast(I32)
         early = [keep.tile([P, PACK, N], F32, name=f"early{u}") for u in range(2)]
-        nc.sync.dma_start(word_table[:], words_in)
+        nc.sync.dma_start(word_table[:, HEAD:], words_in[:, HEAD:])
         load("g", 0, early[0][:], 0, N)
         load("g", 1, early[1][:], 0, N)
 
@@ -118,10 +120,10 @@ def tile_picked_gdconv_none_p_kernel(tc, x_words, x_scales, w1, w2, w3, w4, w5, 
             gate[b] = keep.tile([P, S], F32, name=f"gate{b}", tag=f"gate{b}", align_bytes=64)
             nc.scalar.activation(gate[b][:], acc["g", b][:], mybir.ActivationFunctionType.Sigmoid)
 
-        def finish(b):
-            res = keep.tile([P, S], F32, name=f"res{b}")
-            nc.vector.tensor_tensor(res[:], acc["o", b][:], gate[b][:], mybir.AluOpType.mult)
-            nc.sync.dma_start(out[b * BLOCK : (b + 1) * BLOCK, :], res[:])
+        def finish(b, lo=0, hi=S):
+            res = keep.tile([P, hi - lo], F32, name=f"res{b}_{lo}")
+            nc.vector.tensor_tensor(res[:], acc["o", b][:, lo:hi], gate[b][:, lo:hi], mybir.AluOpType.mult)
+            nc.sync.dma_start(out[b * BLOCK : (b + 1) * BLOCK, lo:hi], res[:])
 
         def step(engine, kind, t, first, count, **tags):
             cast(engine, kind, t, first, count)
@@ -157,5 +159,7 @@ def tile_picked_gdconv_none_p_kernel(tc, x_words, x_scales, w1, w2, w3, w4, w5, 
         step("s", "o", 2, 2, 1)
         stage("last", [("o", 2, 3)])
         step("s", "o", 2, 3, 1)
-        for b in range(4):
+        for b in range(3):
             finish(b)
+        finish(3, 0, HALF)
+        finish(3, HALF, S)

@@ -63,7 +63,7 @@ def tile_picked_gdconv_none_p_kernel(tc, x_words, x_scales, w1, w2, w3, w4, w5, 
             nc.sync.dma_start(x_plane[i:P:32, :].bitcast(I32), picked_scales[8 * i : P : 32, :].bitcast(I32))
         late = keep.tile([P, (TAPS + 1) * PACK * N], F32, name="late", tag="shared", align_bytes=64)
         at = 0
-        for kind, t, lo, width in (("g", 2, 0, N), ("o", 0, 0, N), ("o", 1, 0, N), ("o", 2, 0, HALF), ("o", 2, HALF, BLOCK), ("o", 2, 3 * BLOCK, BLOCK)):
+        for kind, t, lo, width in (("g", 2, 0, N), ("o", 0, 0, N), ("o", 1, 0, HALF), ("o", 2, 0, HALF), ("o", 1, HALF, HALF), ("o", 2, HALF, HALF)):
             load(kind, t, late[:, at : at + PACK * width].rearrange("p (j m) -> p j m", j=PACK), lo, width)
             at = at + PACK * width
 
@@ -121,7 +121,7 @@ def tile_picked_gdconv_none_p_kernel(tc, x_words, x_scales, w1, w2, w3, w4, w5, 
             nc.scalar.activation(gate[b][:], acc["g", b][:], mybir.ActivationFunctionType.Sigmoid)
 
         def finish(b, lo=0, hi=S):
-            res = keep.tile([P, hi - lo], F32, name=f"res{b}_{lo}")
+            res = keep.tile([P, hi - lo], F32, name=f"res{b}_{lo}", tag="scalar_stage2" if b == 1 else f"res{b}_{lo}", align_bytes=64)
             nc.vector.tensor_tensor(res[:], acc["o", b][:, lo:hi], gate[b][:, lo:hi], mybir.AluOpType.mult)
             nc.sync.dma_start(out[b * BLOCK : (b + 1) * BLOCK, lo:hi], res[:])
 
@@ -133,33 +133,41 @@ def tile_picked_gdconv_none_p_kernel(tc, x_words, x_scales, w1, w2, w3, w4, w5, 
 
         for t in range(2):
             if t == 1:
-                pick(2, "bf02")
+                pick(2, "bf00")
             for first in (0, 2):
-                stage("vector_stage" if (t, first) == (1, 2) else f"bf{t}{first}", [("g", t, first), ("g", t, first + 1)])
-                step("s", "g", t, first, 2)
-        stage("vector_stage", [("g", 2, 0), ("g", 2, 1)])
-        stage("bf22", [("g", 2, 2), ("g", 2, 3)])
-        for b in range(3):
-            step("vvs"[b], "g", 2, b, 1, words_tag="tail_c" if b == 2 else "", plane_tag="last" if b == 2 else "")
+                stage(f"bf{t}{first}", [("g", t, first), ("g", t, first + 1)])
+            step("s", "g", t, 0, 2)
+            cast("s", "g", t, 2, 2)
+        stage("bf10", [("g", 2, 0), ("g", 2, 1)])
+        stage("bf22", [("g", 2, 2)])
+        stage("vector_stage", [("g", 2, 3)])
+        for b in range(2):
+            step("v", "g", 2, b, 1)
             sigmoid(b)
-        step("s", "g", 2, 3, 1, words_tag="tail_a", plane_tag="tail_b")
-        sigmoid(3)
-        stage("vector_stage", [("o", 0, b) for b in range(4)])
-        step("v", "o", 0, 0, 2)
-        step("v", "o", 0, 2, 2)
-        stage("vector_stage", [("o", 1, 0), ("o", 1, 1)])
-        stage("tail_b", [("o", 1, 2)])
-        stage("tail_a", [("o", 1, 3), ("o", 2, 1)])
-        stage("tail_c", [("o", 2, 2)])
-        for b in range(4):
-            step("vvss"[b], "o", 1, b, 1)
-        stage("tail_b", [("o", 2, 0)])
-        step("v", "o", 2, 0, 1)
-        step("s", "o", 2, 1, 1)
-        step("s", "o", 2, 2, 1)
-        stage("last", [("o", 2, 3)])
-        step("s", "o", 2, 3, 1)
-        for b in range(3):
-            finish(b)
+        stage_free = ("bf10", "")
+        for t in range(2):
+            quantise("g", t, 2, 2, words_tag=stage_free[t])
+        for b in (2, 3):
+            product("g", 0, b)
+            product("g", 1, b)
+            step("s", "g", 2, b, 1, words_tag=f"scalar_stage{2 * (3 - b)}", plane_tag="scalar_stage1" if b == 3 else "")
+            sigmoid(b)
+        for t in range(2):
+            stage("vector_stage", [("o", t, 0), ("o", t, 1)])
+            step("v", "o", t, 0, 2)
+        stage("vector_stage", [("o", 2, 0), ("o", 2, 1)])
+        for b in range(2):
+            step("v", "o", 2, b, 1)
+        for t in range(2):
+            stage(f"scalar_stage{t}", [("o", t, 2), ("o", t, 3)])
+        step("s", "o", 0, 2, 2, words_tag="vector_stage")
+        finish(0)
+        step("s", "o", 1, 2, 2)
+        for b in (2, 3):
+            stage(f"scalar_stage{b % 3}", [("o", 2, b)])
+            step("s", "o", 2, b, 1)
+            if b == 2:
+                finish(1)
+        finish(2)
         finish(3, 0, HALF)
         finish(3, HALF, S)

@@ -63,7 +63,7 @@ def tile_picked_gdconv_none_p_kernel(tc, x_words, x_scales, w1, w2, w3, w4, w5, 
             nc.sync.dma_start(x_plane[i:P:32, :].bitcast(I32), picked_scales[8 * i : P : 32, :].bitcast(I32))
         late = keep.tile([P, (TAPS + 1) * PACK * N], F32, name="late", tag="shared", align_bytes=64)
         at = 0
-        for kind, t, lo, width in (("g", 2, 0, N), ("o", 0, 0, N), ("o", 1, 0, HALF), ("o", 2, 0, HALF), ("o", 1, HALF, HALF), ("o", 2, HALF, HALF)):
+        for kind, t, lo, width in (("g", 2, 0, N), ("o", 0, 0, N), ("o", 1, 0, 3 * BLOCK), ("o", 2, 0, HALF), ("o", 2, HALF, BLOCK), ("o", 1, 3 * BLOCK, BLOCK), ("o", 2, 3 * BLOCK, BLOCK)):
             load(kind, t, late[:, at : at + PACK * width].rearrange("p (j m) -> p j m", j=PACK), lo, width)
             at = at + PACK * width
 
@@ -77,9 +77,9 @@ def tile_picked_gdconv_none_p_kernel(tc, x_words, x_scales, w1, w2, w3, w4, w5, 
 
         def cast(engine, kind, t, first, count):
             tl, at = rounded[kind, t, first]
-            dst = tl[:, at : at + count * BLOCK, :].rearrange("p (c i) j -> p c j i", i=4)
+            dst = tl[:, at : at + count * BLOCK, :].rearrange("p (c i) j -> p c j i", i=2)
             tl, at = raw[kind, t, first * BLOCK]
-            src = tl[:, :, at : at + count * BLOCK].rearrange("p j (c i) -> p c j i", i=4)
+            src = tl[:, :, at : at + count * BLOCK].rearrange("p j (c i) -> p c j i", i=2)
             if engine == "s":
                 nc.scalar.copy(dst, src)
             else:
@@ -121,7 +121,7 @@ def tile_picked_gdconv_none_p_kernel(tc, x_words, x_scales, w1, w2, w3, w4, w5, 
             nc.scalar.activation(gate[b][:], acc["g", b][:], mybir.ActivationFunctionType.Sigmoid)
 
         def finish(b, lo=0, hi=S):
-            res = keep.tile([P, hi - lo], F32, name=f"res{b}_{lo}", tag="scalar_stage2" if b == 1 else f"res{b}_{lo}", align_bytes=64)
+            res = keep.tile([P, hi - lo], F32, name=f"res{b}_{lo}", tag="bf_o23" if b == 2 else f"res{b}_{lo}", align_bytes=64)
             nc.vector.tensor_tensor(res[:], acc["o", b][:, lo:hi], gate[b][:, lo:hi], mybir.AluOpType.mult)
             nc.sync.dma_start(out[b * BLOCK : (b + 1) * BLOCK, lo:hi], res[:])
 
@@ -150,24 +150,15 @@ def tile_picked_gdconv_none_p_kernel(tc, x_words, x_scales, w1, w2, w3, w4, w5, 
         for b in (2, 3):
             product("g", 0, b)
             product("g", 1, b)
-            step("s", "g", 2, b, 1, words_tag=f"scalar_stage{2 * (3 - b)}", plane_tag="scalar_stage1" if b == 3 else "")
+            step("s", "g", 2, b, 1)
             sigmoid(b)
-        for t in range(2):
-            stage("vector_stage", [("o", t, 0), ("o", t, 1)])
-            step("v", "o", t, 0, 2)
-        stage("vector_stage", [("o", 2, 0), ("o", 2, 1)])
-        for b in range(2):
-            step("v", "o", 2, b, 1)
-        for t in range(2):
-            stage(f"scalar_stage{t}", [("o", t, 2), ("o", t, 3)])
-        step("s", "o", 0, 2, 2, words_tag="vector_stage")
-        finish(0)
-        step("s", "o", 1, 2, 2)
-        for b in (2, 3):
-            stage(f"scalar_stage{b % 3}", [("o", 2, b)])
-            step("s", "o", 2, b, 1)
-            if b == 2:
-                finish(1)
-        finish(2)
+        stage("vector_stage", [("o", 0, b) for b in range(4)])
+        for first in (0, 2):
+            step("v", "o", 0, first, 2)
+        for t, b in ((1, 0), (1, 1), (1, 2), (2, 0), (2, 1), (2, 2), (1, 3), (2, 3)):
+            stage(f"bf_o{t}{b}", [("o", t, b)])
+            step("v" if b < 3 - t else "s", "o", t, b, 1)
+        for b in range(3):
+            finish(b)
         finish(3, 0, HALF)
         finish(3, HALF, S)

@@ -152,12 +152,17 @@ def tile_picked_gdconv_none_p_kernel(tc, x_words, x_scales, w1, w2, w3, w4, w5, 
             product("g", 1, b)
             step("s", "g", 2, b, 1)
             sigmoid(b)
-        stage("vector_stage", [("o", 0, b) for b in range(4)])
-        for first in (0, 2):
-            step("v", "o", 0, first, 2)
-        for t, b in ((1, 0), (1, 1), (1, 2), (2, 0), (2, 1), (2, 2), (1, 3), (2, 3)):
+        stage("vector_stage", [("o", 0, b) for b in range(3)])
+        cast("v", "o", 0, 0, 2)
+        cast("v", "o", 0, 2, 1)
+        for first, count in ((0, 2), (2, 1)):
+            quantise("o", 0, first, count)
+            for b in range(first, first + count):
+                product("o", 0, b)
+        freed = {(1, 2): "bf_o20", (0, 3): "bf_o21"}
+        for t, b in ((1, 0), (1, 1), (2, 0), (1, 2), (2, 1), (0, 3), (2, 2), (1, 3), (2, 3)):
             stage(f"bf_o{t}{b}", [("o", t, b)])
-            step("v" if b < 3 - t else "s", "o", t, b, 1)
+            step("v" if b < 3 - t else "s", "o", t, b, 1, words_tag=freed.get((t, b), ""))
         for b in range(3):
             finish(b)
         finish(3, 0, HALF)

@@ -16,6 +16,7 @@ K, T, S, N = 512, 2048, 512, 512
 TAPS = 3
 HALF = 256
 BLOCK = 128
+BLOCKS = N // BLOCK
 HEAD = 512
 FLOPS = 2 * 2 * TAPS * K * N * S
 
@@ -46,15 +47,16 @@ def tile_picked_gdconv_none_p_kernel(tc, x_words, x_scales, w1, w2, w3, w4, w5, 
         weights = {"g": (w4, w5, w6), "o": (w1, w2, w3)}
         raw = {}
 
-        def load(kind, t, tl, lo, width):
-            nc.sync.dma_start(tl, weights[kind][t].rearrange("(p j) m -> p j m", j=PACK)[:, :, lo : lo + width])
-            for b in range(width // BLOCK):
-                raw[kind, t, lo + b * BLOCK] = (tl, b * BLOCK)
+        def load(kind, t, tl, first, count):
+            lo, hi = first * BLOCK, (first + count) * BLOCK
+            nc.sync.dma_start(tl, weights[kind][t].rearrange("(p j) m -> p j m", j=PACK)[:, :, lo:hi])
+            for b in range(count):
+                raw[kind, t, first + b] = (tl, b * BLOCK)
 
         early = [keep.tile([P, PACK, N], F32, name=f"early{u}") for u in range(2)]
+        load("g", 0, early[0][:], 0, BLOCKS)
         nc.sync.dma_start(word_table[:, HEAD:], words_in[:, HEAD:])
-        load("g", 0, early[0][:], 0, N)
-        load("g", 1, early[1][:], 0, N)
+        load("g", 1, early[1][:], 0, BLOCKS)
 
         picked_scales = keep.tile([P, TAPS * S], U8, name="picked_scales", align_bytes=64)
         for t in range(TAPS):
@@ -63,107 +65,78 @@ def tile_picked_gdconv_none_p_kernel(tc, x_words, x_scales, w1, w2, w3, w4, w5, 
             nc.sync.dma_start(x_plane[i:P:32, :].bitcast(I32), picked_scales[8 * i : P : 32, :].bitcast(I32))
         late = keep.tile([P, (TAPS + 1) * PACK * N], F32, name="late", tag="shared", align_bytes=64)
         at = 0
-        for kind, t, lo, width in (("g", 2, 0, N), ("o", 0, 0, N), ("o", 1, 0, 3 * BLOCK), ("o", 2, 0, HALF), ("o", 2, HALF, BLOCK), ("o", 1, 3 * BLOCK, BLOCK), ("o", 2, 3 * BLOCK, BLOCK)):
-            load(kind, t, late[:, at : at + PACK * width].rearrange("p (j m) -> p j m", j=PACK), lo, width)
-            at = at + PACK * width
+        for kind, t, first, count in [("g", 2, 0, BLOCKS), ("o", 0, 0, BLOCKS), ("o", 1, 0, BLOCKS)] + [("o", 2, b, 1) for b in range(BLOCKS)]:
+            size = PACK * count * BLOCK
+            load(kind, t, late[:, at : at + size].rearrange("p (j m) -> p j m", j=PACK), first, count)
+            at = at + size
 
-        codes = {}
+        picked = {}
+        for t in range(TAPS):
+            picked[t] = keep.tile([P, S], U32, name=f"picked{t}", align_bytes=64)
+            nc.vector.tensor_copy(picked[t][:], word_table[:].bitcast(U32).indirect(lists[t][:]))
+
+        acc = {}
+        for kind in ("g", "o"):
+            for b in range(BLOCKS):
+                acc[kind, b] = psum.tile([P, S], F32, name=f"acc_{kind}{b}")
+
         rounded = {}
 
-        def stage(tag, pieces):
-            tl = keep.tile([P, len(pieces) * BLOCK, PACK], BF16, name="bf_%s%d%d" % pieces[0], tag=tag, align_bytes=64)
-            for n, piece in enumerate(pieces):
-                rounded[piece] = (tl, n * BLOCK)
-
         def cast(engine, kind, t, first, count):
-            tl, at = rounded[kind, t, first]
-            dst = tl[:, at : at + count * BLOCK, :].rearrange("p (c i) j -> p c j i", i=2)
-            tl, at = raw[kind, t, first * BLOCK]
+            stage = keep.tile([P, count * BLOCK, PACK], BF16, name=f"bf_{kind}{t}{first}", align_bytes=64)
+            rounded[kind, t, first] = stage
+            dst = stage[:].rearrange("p (c i) j -> p c j i", i=2)
+            tl, at = raw[kind, t, first]
             src = tl[:, :, at : at + count * BLOCK].rearrange("p j (c i) -> p c j i", i=2)
             if engine == "s":
                 nc.scalar.copy(dst, src)
             else:
                 nc.vector.tensor_copy(dst, src)
 
-        def quantise(kind, t, first, count, words_tag="", plane_tag=""):
+        def multiply(kind, t, first, count):
             width = count * BLOCK
-            words = keep.tile([P, width], U32, name=f"q_{kind}{t}{first}", tag=words_tag or f"q_{kind}{t}{first}", align_bytes=64)
-            plane = keep.tile([P, width], U8, name=f"s_{kind}{t}{first}", tag=plane_tag or f"s_{kind}{t}{first}", align_bytes=64)
-            tl, at = rounded[kind, t, first]
-            nc.vector.quantize_mx(out=words[:].bitcast(FP8X4), scales=plane[:], in_=tl[:, at : at + width, :].rearrange("p c j -> p (c j)"))
+            words = keep.tile([P, width], U32, name=f"q_{kind}{t}{first}", align_bytes=64)
+            plane = keep.tile([P, width], U8, name=f"s_{kind}{t}{first}", align_bytes=64)
+            nc.vector.quantize_mx(out=words[:].bitcast(FP8X4), scales=plane[:], in_=rounded[kind, t, first][:].rearrange("p c j -> p (c j)"))
             for b in range(count):
-                codes[kind, t, first + b] = (words[:, b * BLOCK : (b + 1) * BLOCK], plane[:, b * BLOCK : (b + 1) * BLOCK])
-
-        picked = {}
-
-        def pick(t, tag):
-            picked[t] = keep.tile([P, S], U32, name=f"picked{t}", tag=tag, align_bytes=64)
-            nc.vector.tensor_copy(picked[t][:], word_table[:].bitcast(U32).indirect(lists[t][:]))
-
-        pick(0, "picked0")
-        pick(1, "picked1")
-
-        acc = {}
-        for kind in ("g", "o"):
-            for b in range(4):
-                acc[kind, b] = psum.tile([P, S], F32, name=f"acc_{kind}{b}")
-
-        def product(kind, t, b):
-            words, plane = codes[kind, t, b]
-            nc.tensor.matmul_mx(out=acc[kind, b][:], lhsT=words.bitcast(FP8X4), lhsT_scale=plane,
-                                rhs=picked[t][:].bitcast(FP8X4), rhs_scale=x_plane[:, t * S : (t + 1) * S],
-                                start=(t == 0), stop=(t == TAPS - 1))
+                cols = slice(b * BLOCK, (b + 1) * BLOCK)
+                nc.tensor.matmul_mx(out=acc[kind, first + b][:], lhsT=words[:, cols].bitcast(FP8X4), lhsT_scale=plane[:, cols],
+                                    rhs=picked[t][:].bitcast(FP8X4), rhs_scale=x_plane[:, t * S : (t + 1) * S],
+                                    start=(t == 0), stop=(t == TAPS - 1))
 
         gate = {}
 
         def sigmoid(b):
-            gate[b] = keep.tile([P, S], F32, name=f"gate{b}", tag=f"gate{b}", align_bytes=64)
+            gate[b] = keep.tile([P, S], F32, name=f"gate{b}", align_bytes=64)
             nc.scalar.activation(gate[b][:], acc["g", b][:], mybir.ActivationFunctionType.Sigmoid)
 
         def finish(b, lo=0, hi=S):
-            res = keep.tile([P, hi - lo], F32, name=f"res{b}_{lo}", tag="bf_o23" if b == 2 else f"res{b}_{lo}", align_bytes=64)
+            res = keep.tile([P, hi - lo], F32, name=f"res{b}_{lo}", align_bytes=64)
             nc.vector.tensor_tensor(res[:], acc["o", b][:, lo:hi], gate[b][:, lo:hi], mybir.AluOpType.mult)
             nc.sync.dma_start(out[b * BLOCK : (b + 1) * BLOCK, lo:hi], res[:])
 
-        def step(engine, kind, t, first, count, **tags):
-            cast(engine, kind, t, first, count)
-            quantise(kind, t, first, count, **tags)
-            for b in range(first, first + count):
-                product(kind, t, b)
-
         for t in range(2):
-            if t == 1:
-                pick(2, "bf00")
             for first in (0, 2):
-                stage(f"bf{t}{first}", [("g", t, first), ("g", t, first + 1)])
-            step("s", "g", t, 0, 2)
-            cast("s", "g", t, 2, 2)
-        stage("bf10", [("g", 2, 0), ("g", 2, 1)])
-        stage("bf22", [("g", 2, 2)])
-        stage("vector_stage", [("g", 2, 3)])
-        for b in range(2):
-            step("v", "g", 2, b, 1)
+                cast("s", "g", t, first, 2)
+                multiply("g", t, first, 2)
+        for b in range(BLOCKS):
+            cast("v" if b < 2 else "s", "g", 2, b, 1)
+        for b in (0, 2, 1, 3):
+            multiply("g", 2, b, 1)
             sigmoid(b)
-        stage_free = ("bf10", "")
-        for t in range(2):
-            quantise("g", t, 2, 2, words_tag=stage_free[t])
-        for b in (2, 3):
-            product("g", 0, b)
-            product("g", 1, b)
-            step("s", "g", 2, b, 1)
-            sigmoid(b)
-        stage("vector_stage", [("o", 0, b) for b in range(3)])
-        cast("v", "o", 0, 0, 2)
-        cast("v", "o", 0, 2, 1)
-        for first, count in ((0, 2), (2, 1)):
-            quantise("o", 0, first, count)
-            for b in range(first, first + count):
-                product("o", 0, b)
-        freed = {(1, 2): "bf_o20", (0, 3): "bf_o21"}
-        for t, b in ((1, 0), (1, 1), (2, 0), (1, 2), (2, 1), (0, 3), (2, 2), (1, 3), (2, 3)):
-            stage(f"bf_o{t}{b}", [("o", t, b)])
-            step("v" if b < 3 - t else "s", "o", t, b, 1, words_tag=freed.get((t, b), ""))
-        for b in range(3):
-            finish(b)
+        for first in (0, 2):
+            cast("v", "o", 0, first, 2)
+        for first in (0, 2):
+            multiply("o", 0, first, 2)
+        for b in range(BLOCKS):
+            cast("v" if b < 2 else "s", "o", 1, b, 1)
+        multiply("o", 1, 0, 1)
+        for b in range(BLOCKS):
+            cast("v" if b < 1 else "s", "o", 2, b, 1)
+            if b + 1 < BLOCKS:
+                multiply("o", 1, b + 1, 1)
+            multiply("o", 2, b, 1)
+            if b > 0:
+                finish(b - 1)
         finish(3, 0, HALF)
         finish(3, HALF, S)

@@ -27,9 +27,9 @@ def tile_picked_gdconv_none_p_kernel(tc, x_words, x_scales, w1, w2, w3, w4, w5, 
         keep = ctx.enter_context(tc.tile_pool(name="keep", bufs=1))
         psum = ctx.enter_context(tc.psum_pool(name="psum", bufs=1))
 
-        scale_table = keep.tile([P, T], U8, name="scale_table", tag="shared", align_bytes=64)
+        scale_table = keep.tile([P, T], U8, name="scale_table", tag="shared", align_bytes=256)
         nc.gpsimd.memset(scale_table[:].bitcast(I32), 0)
-        word_table = keep.tile([P, T], I32, name="word_table", align_bytes=64)
+        word_table = keep.tile([P, T], I32, name="word_table", align_bytes=256)
         words_in = x_words[0].rearrange("p n t -> p (n t)").bitcast(I32)
         nc.sync.dma_start(word_table[:, :HEAD], words_in[:, :HEAD])
         lists = []
@@ -37,11 +37,11 @@ def tile_picked_gdconv_none_p_kernel(tc, x_words, x_scales, w1, w2, w3, w4, w5, 
             tl = keep.tile([P, S // 16], U16, name=f"list{t}")
             nc.sync.dma_start(tl[:], src)
             lists.append(tl)
-        nc.sync.dma_start(scale_table[0:P:8, :].bitcast(I32), x_scales[0].bitcast(I32))
+        nc.sync.dma_start(scale_table[4:P:8, :].bitcast(I32), x_scales[0].bitcast(I32))
         warm = keep.tile([P, 16], F32, name="warm")
         nc.gpsimd.memset(warm[:, 0:1], 0.0)
         nc.scalar.activation(warm[:, 8:9], warm[:, 0:1], mybir.ActivationFunctionType.Sigmoid)
-        x_plane = keep.tile([P, TAPS * S], U8, name="x_plane", align_bytes=64)
+        x_plane = keep.tile([P, TAPS * S], U8, name="x_plane", align_bytes=256)
         nc.gpsimd.memset(x_plane[:].bitcast(I32), 0)
 
         weights = {"g": (w4, w5, w6), "o": (w1, w2, w3)}
@@ -53,17 +53,17 @@ def tile_picked_gdconv_none_p_kernel(tc, x_words, x_scales, w1, w2, w3, w4, w5, 
             for b in range(count):
                 raw[kind, t, first + b] = (tl, b * BLOCK)
 
-        early = [keep.tile([P, PACK, N], F32, name=f"early{u}") for u in range(2)]
+        early = [keep.tile([P, PACK, N], F32, name=f"early{u}", align_bytes=256) for u in range(2)]
         load("g", 0, early[0][:], 0, BLOCKS)
         nc.sync.dma_start(word_table[:, HEAD:], words_in[:, HEAD:])
         load("g", 1, early[1][:], 0, BLOCKS)
 
-        picked_scales = keep.tile([P, TAPS * S], U8, name="picked_scales", align_bytes=64)
+        picked_scales = keep.tile([P, TAPS * S], U8, name="picked_scales", align_bytes=256)
         for t in range(TAPS):
             nc.vector.tensor_copy(picked_scales[:, t * S : (t + 1) * S], scale_table[:].indirect(lists[t][:]))
         for i in range(4):
-            nc.sync.dma_start(x_plane[i:P:32, :].bitcast(I32), picked_scales[8 * i : P : 32, :].bitcast(I32))
-        late = keep.tile([P, (TAPS + 1) * PACK * N], F32, name="late", tag="shared", align_bytes=64)
+            nc.sync.dma_start(x_plane[i:P:32, :].bitcast(I32), picked_scales[8 * i + 4 : P : 32, :].bitcast(I32))
+        late = keep.tile([P, (TAPS + 1) * PACK * N], F32, name="late", tag="shared", align_bytes=256)
         at = 0
         for kind, t, first, count in [("g", 2, 0, BLOCKS), ("o", 0, 0, BLOCKS), ("o", 1, 0, BLOCKS)] + [("o", 2, b, 1) for b in range(BLOCKS)]:
             size = PACK * count * BLOCK
@@ -111,7 +111,7 @@ def tile_picked_gdconv_none_p_kernel(tc, x_words, x_scales, w1, w2, w3, w4, w5, 
             nc.scalar.activation(gate[b][:], acc["g", b][:], mybir.ActivationFunctionType.Sigmoid)
 
         def finish(b, lo=0, hi=S):
-            res = keep.tile([P, hi - lo], F32, name=f"res{b}_{lo}", align_bytes=64)
+            res = keep.tile([P, hi - lo], F32, name=f"res{b}_{lo}", align_bytes=256)
             nc.vector.tensor_tensor(res[:], acc["o", b][:, lo:hi], gate[b][:, lo:hi], mybir.AluOpType.mult)
             nc.sync.dma_start(out[b * BLOCK : (b + 1) * BLOCK, lo:hi], res[:])
 

@@ -34,7 +34,7 @@ def tile_picked_gdconv_none_p_kernel(tc, x_words, x_scales, w1, w2, w3, w4, w5, 
         nc.sync.dma_start(word_table[:, :HEAD], words_in[:, :HEAD])
         lists = []
         for t, src in enumerate((offs, tap1, tap2)):
-            tl = keep.tile([P, S // 16], U16, name=f"list{t}")
+            tl = keep.tile([P, S // 16], U16, name=f"list{t}", align_bytes=256)
             nc.sync.dma_start(tl[:], src)
             lists.append(tl)
         nc.sync.dma_start(scale_table[4:P:8, :].bitcast(I32), x_scales[0].bitcast(I32))
@@ -72,7 +72,7 @@ def tile_picked_gdconv_none_p_kernel(tc, x_words, x_scales, w1, w2, w3, w4, w5, 
 
         picked = {}
         for t in range(TAPS):
-            picked[t] = keep.tile([P, S], U32, name=f"picked{t}", align_bytes=64)
+            picked[t] = keep.tile([P, S], U32, name=f"picked{t}", align_bytes=256)
             nc.vector.tensor_copy(picked[t][:], word_table[:].bitcast(U32).indirect(lists[t][:]))
 
         acc = {}
@@ -83,7 +83,7 @@ def tile_picked_gdconv_none_p_kernel(tc, x_words, x_scales, w1, w2, w3, w4, w5, 
         rounded = {}
 
         def cast(engine, kind, t, first, count):
-            stage = keep.tile([P, count * BLOCK, PACK], BF16, name=f"bf_{kind}{t}{first}", align_bytes=64)
+            stage = keep.tile([P, count * BLOCK, PACK], BF16, name=f"bf_{kind}{t}{first}", align_bytes=256)
             rounded[kind, t, first] = stage
             dst = stage[:].rearrange("p (c i) j -> p c j i", i=2)
             tl, at = raw[kind, t, first]
@@ -95,8 +95,8 @@ def tile_picked_gdconv_none_p_kernel(tc, x_words, x_scales, w1, w2, w3, w4, w5, 
 
         def multiply(kind, t, first, count):
             width = count * BLOCK
-            words = keep.tile([P, width], U32, name=f"q_{kind}{t}{first}", align_bytes=64)
-            plane = keep.tile([P, width], U8, name=f"s_{kind}{t}{first}", align_bytes=64)
+            words = keep.tile([P, width], U32, name=f"q_{kind}{t}{first}", align_bytes=256)
+            plane = keep.tile([P, width], U8, name=f"s_{kind}{t}{first}", align_bytes=256)
             nc.vector.quantize_mx(out=words[:].bitcast(FP8X4), scales=plane[:], in_=rounded[kind, t, first][:].rearrange("p c j -> p (c j)"))
             for b in range(count):
                 cols = slice(b * BLOCK, (b + 1) * BLOCK)
@@ -107,7 +107,7 @@ def tile_picked_gdconv_none_p_kernel(tc, x_words, x_scales, w1, w2, w3, w4, w5, 
         gate = {}
 
         def sigmoid(b):
-            gate[b] = keep.tile([P, S], F32, name=f"gate{b}", align_bytes=64)
+            gate[b] = keep.tile([P, S], F32, name=f"gate{b}", align_bytes=256)
             nc.scalar.activation(gate[b][:], acc["g", b][:], mybir.ActivationFunctionType.Sigmoid)
 
         def finish(b, lo=0, hi=S):

@@ -85,9 +85,9 @@ def tile_picked_gdconv_none_p_kernel(tc, x_words, x_scales, w1, w2, w3, w4, w5, 
         def cast(engine, kind, t, first, count):
             stage = keep.tile([P, count * BLOCK, PACK], BF16, name=f"bf_{kind}{t}{first}", align_bytes=256)
             rounded[kind, t, first] = stage
-            dst = stage[:].rearrange("p (c i) j -> p c j i", i=2)
+            dst = stage[:].rearrange("p (c i) j -> p c j i", i=4)
             tl, at = raw[kind, t, first]
-            src = tl[:, :, at : at + count * BLOCK].rearrange("p j (c i) -> p c j i", i=2)
+            src = tl[:, :, at : at + count * BLOCK].rearrange("p j (c i) -> p c j i", i=4)
             if engine == "s":
                 nc.scalar.copy(dst, src)
             else:

@@ -71,8 +71,9 @@ def tile_picked_gdconv_none_p_kernel(tc, x_words, x_scales, w1, w2, w3, w4, w5, 
             at = at + size
 
         picked = {}
-        for t in range(TAPS):
-            picked[t] = keep.tile([P, S], U32, name=f"picked{t}", align_bytes=256)
+
+        def pick(t, tag):
+            picked[t] = keep.tile([P, S], U32, name=f"picked{t}", tag=tag, align_bytes=256)
             nc.vector.tensor_copy(picked[t][:], word_table[:].bitcast(U32).indirect(lists[t][:]))
 
         acc = {}
@@ -115,10 +116,15 @@ def tile_picked_gdconv_none_p_kernel(tc, x_words, x_scales, w1, w2, w3, w4, w5, 
             nc.vector.tensor_tensor(res[:], acc["o", b][:, lo:hi], gate[b][:, lo:hi], mybir.AluOpType.mult)
             nc.sync.dma_start(out[b * BLOCK : (b + 1) * BLOCK, lo:hi], res[:])
 
-        for t in range(2):
-            for first in (0, 2):
-                cast("s", "g", t, first, 2)
-                multiply("g", t, first, 2)
+        pick(0, "picked0")
+        for first in (0, 2):
+            cast("s", "g", 0, first, 2)
+            multiply("g", 0, first, 2)
+        pick(1, "bf_g02")
+        pick(2, "picked2")
+        for first in (0, 2):
+            cast("s", "g", 1, first, 2)
+            multiply("g", 1, first, 2)
         for b in range(BLOCKS):
             cast("v" if b < 2 else "s", "g", 2, b, 1)
         for b in (0, 2, 1, 3):

@@ -18,6 +18,10 @@ HALF = 256
 BLOCK = 128
 BLOCKS = N // BLOCK
 HEAD = 512
+RUN = 4
+ALIGN = 256
+TABLE_ROW = 4
+RAW_BYTES = PACK * N * 4
 FLOPS = 2 * 2 * TAPS * K * N * S
 
 
@@ -26,54 +30,61 @@ def tile_picked_gdconv_none_p_kernel(tc, x_words, x_scales, w1, w2, w3, w4, w5, 
     with ExitStack() as ctx:
         keep = ctx.enter_context(tc.tile_pool(name="keep", bufs=1))
         psum = ctx.enter_context(tc.psum_pool(name="psum", bufs=1))
+        reuse = ctx.enter_context(tc.tile_pool(name="reuse", bufs=1))
 
-        scale_table = keep.tile([P, T], U8, name="scale_table", tag="shared", align_bytes=256)
+        scale_table = keep.tile([P, T], U8, name="scale_table", tag="shared", align_bytes=ALIGN)
         nc.gpsimd.memset(scale_table[:].bitcast(I32), 0)
-        word_table = keep.tile([P, T], I32, name="word_table", align_bytes=256)
+        word_table = keep.tile([P, T], I32, name="word_table", align_bytes=ALIGN)
         words_in = x_words[0].rearrange("p n t -> p (n t)").bitcast(I32)
         nc.sync.dma_start(word_table[:, :HEAD], words_in[:, :HEAD])
         lists = []
         for t, src in enumerate((offs, tap1, tap2)):
-            tl = keep.tile([P, S // 16], U16, name=f"list{t}", align_bytes=256)
-            nc.sync.dma_start(tl[:], src)
-            lists.append(tl)
-        nc.sync.dma_start(scale_table[4:P:8, :].bitcast(I32), x_scales[0].bitcast(I32))
+            offsets = keep.tile([P, S // 16], U16, name=f"list{t}", align_bytes=ALIGN)
+            nc.sync.dma_start(offsets[:], src)
+            lists.append(offsets)
+        nc.sync.dma_start(scale_table[TABLE_ROW:P:8, :].bitcast(I32), x_scales[0].bitcast(I32))
         warm = keep.tile([P, 16], F32, name="warm")
         nc.gpsimd.memset(warm[:, 0:1], 0.0)
         nc.scalar.activation(warm[:, 8:9], warm[:, 0:1], mybir.ActivationFunctionType.Sigmoid)
-        x_plane = keep.tile([P, TAPS * S], U8, name="x_plane", align_bytes=256)
+        x_plane = keep.tile([P, TAPS * S], U8, name="x_plane", align_bytes=ALIGN)
         nc.gpsimd.memset(x_plane[:].bitcast(I32), 0)
 
         weights = {"g": (w4, w5, w6), "o": (w1, w2, w3)}
         raw = {}
 
-        def load(kind, t, tl, first, count):
+        def load(kind, t, piece, first, count):
             lo, hi = first * BLOCK, (first + count) * BLOCK
-            nc.sync.dma_start(tl, weights[kind][t].rearrange("(p j) m -> p j m", j=PACK)[:, :, lo:hi])
+            nc.sync.dma_start(piece, weights[kind][t].rearrange("(p j) m -> p j m", j=PACK)[:, :, lo:hi])
             for b in range(count):
-                raw[kind, t, first + b] = (tl, b * BLOCK)
+                raw[kind, t, first + b] = (piece, b * BLOCK)
 
-        early = [keep.tile([P, PACK, N], F32, name=f"early{u}", align_bytes=256) for u in range(2)]
+        early = [reuse.tile([P, PACK, N], F32, name=f"early{u}", offset=RAW_BYTES * u, align_bytes=ALIGN) for u in range(2)]
         load("g", 0, early[0][:], 0, BLOCKS)
         nc.sync.dma_start(word_table[:, HEAD:], words_in[:, HEAD:])
         load("g", 1, early[1][:], 0, BLOCKS)
 
-        picked_scales = keep.tile([P, TAPS * S], U8, name="picked_scales", align_bytes=256)
+        picked_scales = keep.tile([P, TAPS * S], U8, name="picked_scales", align_bytes=ALIGN)
         for t in range(TAPS):
             nc.vector.tensor_copy(picked_scales[:, t * S : (t + 1) * S], scale_table[:].indirect(lists[t][:]))
         for i in range(4):
-            nc.sync.dma_start(x_plane[i:P:32, :].bitcast(I32), picked_scales[8 * i + 4 : P : 32, :].bitcast(I32))
-        late = keep.tile([P, (TAPS + 1) * PACK * N], F32, name="late", tag="shared", align_bytes=256)
+            nc.sync.dma_start(x_plane[i:P:32, :].bitcast(I32), picked_scales[8 * i + TABLE_ROW : P : 32, :].bitcast(I32))
+        late = keep.tile([P, 15 * PACK * BLOCK], F32, name="late", tag="shared", align_bytes=ALIGN)
         at = 0
-        for kind, t, first, count in [("g", 2, 0, BLOCKS), ("o", 0, 0, BLOCKS), ("o", 1, 0, BLOCKS)] + [("o", 2, b, 1) for b in range(BLOCKS)]:
+        spot = {}
+        for kind, t, first, count, where in [("g", 2, 0, 4, None), ("o", 0, 0, 4, None), ("o", 1, 0, 4, None)] + [("o", 2, b, 1, 0 if b == 1 else None) for b in range(BLOCKS)]:
             size = PACK * count * BLOCK
-            load(kind, t, late[:, at : at + size].rearrange("p (j m) -> p j m", j=PACK), first, count)
-            at = at + size
+            if where is None:
+                load(kind, t, late[:, at : at + size].rearrange("p (j m) -> p j m", j=PACK), first, count)
+                spot[kind, t, first] = at
+                at = at + size
+            else:
+                piece = reuse.tile([P, PACK, count * BLOCK], F32, name=f"raw_{kind}{t}{first}", offset=where, align_bytes=ALIGN)
+                load(kind, t, piece[:], first, count)
 
         picked = {}
 
         def pick(t, tag):
-            picked[t] = keep.tile([P, S], U32, name=f"picked{t}", tag=tag, align_bytes=256)
+            picked[t] = keep.tile([P, S], U32, name=f"picked{t}", tag=tag, align_bytes=ALIGN)
             nc.vector.tensor_copy(picked[t][:], word_table[:].bitcast(U32).indirect(lists[t][:]))
 
         acc = {}
@@ -83,38 +94,64 @@ def tile_picked_gdconv_none_p_kernel(tc, x_words, x_scales, w1, w2, w3, w4, w5, 
 
         rounded = {}
 
-        def cast(engine, kind, t, first, count):
-            stage = keep.tile([P, count * BLOCK, PACK], BF16, name=f"bf_{kind}{t}{first}", align_bytes=256)
-            rounded[kind, t, first] = stage
-            dst = stage[:].rearrange("p (c i) j -> p c j i", i=4)
-            tl, at = raw[kind, t, first]
-            src = tl[:, :, at : at + count * BLOCK].rearrange("p j (c i) -> p c j i", i=4)
-            if engine == "s":
-                nc.scalar.copy(dst, src)
-            else:
-                nc.vector.tensor_copy(dst, src)
+        def place(shape, dtype, name, where):
+            if where is None:
+                return keep.tile(shape, dtype, name=name, align_bytes=ALIGN)
+            return reuse.tile(shape, dtype, name=name, offset=where, align_bytes=ALIGN)
 
-        def multiply(kind, t, first, count):
+        def cast(engines, kind, t, first, count):
+            stage = keep.tile([P, count * BLOCK, PACK], BF16, name=f"bf_{kind}{t}{first}", align_bytes=ALIGN)
+            for b in range(count):
+                rounded[kind, t, first + b] = (stage, b * BLOCK)
+            piece, at = raw[kind, t, first]
+            share = count * BLOCK // len(engines)
+            for u, engine in enumerate(engines):
+                dst = stage[:, u * share : (u + 1) * share, :].rearrange("p (c i) j -> p c j i", i=RUN)
+                src = piece[:, :, at + u * share : at + (u + 1) * share].rearrange("p j (c i) -> p c j i", i=RUN)
+                if engine == "s":
+                    nc.scalar.copy(dst, src)
+                else:
+                    nc.vector.tensor_copy(dst, src)
+
+        codes = {}
+        passes = {}
+
+        def quantise(kind, t, first, count, where=None):
             width = count * BLOCK
-            words = keep.tile([P, width], U32, name=f"q_{kind}{t}{first}", align_bytes=256)
-            plane = keep.tile([P, width], U8, name=f"s_{kind}{t}{first}", align_bytes=256)
-            nc.vector.quantize_mx(out=words[:].bitcast(FP8X4), scales=plane[:], in_=rounded[kind, t, first][:].rearrange("p c j -> p (c j)"))
+            words = keep.tile([P, width], U32, name=f"q_{kind}{t}{first}", align_bytes=ALIGN)
+            plane = place([P, width], U8, f"s_{kind}{t}{first}", where)
+            stage, at = rounded[kind, t, first]
+            nc.vector.quantize_mx(out=words[:].bitcast(FP8X4), scales=plane[:], in_=stage[:, at : at + width, :].rearrange("p c j -> p (c j)"))
             for b in range(count):
                 cols = slice(b * BLOCK, (b + 1) * BLOCK)
-                nc.tensor.matmul_mx(out=acc[kind, first + b][:], lhsT=words[:, cols].bitcast(FP8X4), lhsT_scale=plane[:, cols],
-                                    rhs=picked[t][:].bitcast(FP8X4), rhs_scale=x_plane[:, t * S : (t + 1) * S],
-                                    start=(t == 0), stop=(t == TAPS - 1))
+                codes[kind, t, first + b] = (words[:, cols], plane[:, cols])
+
+        def matmul(kind, t, b):
+            words, plane = codes[kind, t, b]
+            seen = passes.get((kind, b), 0)
+            passes[kind, b] = seen + 1
+            nc.tensor.matmul_mx(out=acc[kind, b][:], lhsT=words.bitcast(FP8X4), lhsT_scale=plane,
+                                rhs=picked[t][:].bitcast(FP8X4), rhs_scale=x_plane[:, t * S : (t + 1) * S],
+                                start=(seen == 0), stop=(seen == TAPS - 1))
+
+        def multiply(kind, t, first, count, where=None):
+            quantise(kind, t, first, count, where)
+            for b in range(first, first + count):
+                matmul(kind, t, b)
 
         gate = {}
 
-        def sigmoid(b):
-            gate[b] = keep.tile([P, S], F32, name=f"gate{b}", align_bytes=256)
+        def sigmoid(b, where=None):
+            gate[b] = place([P, S], F32, f"gate{b}", where)
             nc.scalar.activation(gate[b][:], acc["g", b][:], mybir.ActivationFunctionType.Sigmoid)
 
-        def finish(b, lo=0, hi=S):
-            res = keep.tile([P, hi - lo], F32, name=f"res{b}_{lo}", align_bytes=256)
-            nc.vector.tensor_tensor(res[:], acc["o", b][:, lo:hi], gate[b][:, lo:hi], mybir.AluOpType.mult)
-            nc.sync.dma_start(out[b * BLOCK : (b + 1) * BLOCK, lo:hi], res[:])
+        def finish(b, lo=0, hi=S, over=None):
+            if over is None:
+                res = keep.tile([P, hi - lo], F32, name=f"res{b}_{lo}", align_bytes=ALIGN)[:]
+            else:
+                res = late[:, over : over + hi - lo]
+            nc.vector.tensor_tensor(res, acc["o", b][:, lo:hi], gate[b][:, lo:hi], mybir.AluOpType.mult)
+            nc.sync.dma_start(out[b * BLOCK : (b + 1) * BLOCK, lo:hi], res)
 
         pick(0, "picked0")
         for first in (0, 2):
@@ -122,27 +159,36 @@ def tile_picked_gdconv_none_p_kernel(tc, x_words, x_scales, w1, w2, w3, w4, w5, 
             multiply("g", 0, first, 2)
         pick(1, "bf_g02")
         pick(2, "picked2")
-        for first in (0, 2):
-            cast("s", "g", 1, first, 2)
-            multiply("g", 1, first, 2)
+        cast("s", "g", 1, 0, 2)
+        multiply("g", 1, 0, 2)
+        cast("s", "g", 1, 2, 2)
+        quantise("g", 1, 2, 2)
         for b in range(BLOCKS):
             cast("v" if b < 2 else "s", "g", 2, b, 1)
-        for b in (0, 2, 1, 3):
+        for b in range(BLOCKS):
             multiply("g", 2, b, 1)
+            if b >= 2:
+                matmul("g", 1, b)
+        for b in range(BLOCKS):
             sigmoid(b)
         for first in (0, 2):
             cast("v", "o", 0, first, 2)
         for first in (0, 2):
             multiply("o", 0, first, 2)
-        for b in range(BLOCKS):
-            cast("v" if b < 2 else "s", "o", 1, b, 1)
-        multiply("o", 1, 0, 1)
+        cast("v", "o", 1, 0, 2)
+        cast("s", "o", 1, 2, 2)
         for b in range(BLOCKS):
             cast("v" if b < 1 else "s", "o", 2, b, 1)
-            if b + 1 < BLOCKS:
-                multiply("o", 1, b + 1, 1)
-            multiply("o", 2, b, 1)
-            if b > 0:
-                finish(b - 1)
+        multiply("o", 1, 0, 1)
+        multiply("o", 2, 0, 1)
+        multiply("o", 1, 1, 1)
+        multiply("o", 1, 2, 1)
+        multiply("o", 2, 1, 1)
+        multiply("o", 1, 3, 1, 0)
+        finish(0)
+        multiply("o", 2, 2, 1)
+        finish(1)
+        multiply("o", 2, 3, 1)
+        finish(2)
         finish(3, 0, HALF)
         finish(3, HALF, S)

from contextlib import ExitStack

import concourse.mybir as mybir

F32 = mybir.dt.float32
BF16 = mybir.dt.bfloat16
I32 = mybir.dt.int32
U32 = mybir.dt.uint32
U16 = mybir.dt.uint16
U8 = mybir.dt.uint8
FP8X4 = mybir.dt.float8_e4m3fn_x4

P = 128
PACK = 4
K, T, S, N = 512, 2048, 512, 512
TAPS = 3
HALF = 256
BLOCK = 128
BLOCKS = N // BLOCK
HEAD = 512
RUN = 4
ALIGN = 256
TABLE_ROW = 4
RAW_BYTES = PACK * N * 4
FLOPS = 2 * 2 * TAPS * K * N * S


def tile_picked_gdconv_none_p_kernel(tc, x_words, x_scales, w1, w2, w3, w4, w5, w6, offs, tap1, tap2, out):
    nc = tc.nc
    with ExitStack() as ctx:
        keep = ctx.enter_context(tc.tile_pool(name="keep", bufs=1))
        psum = ctx.enter_context(tc.psum_pool(name="psum", bufs=1))
        reuse = ctx.enter_context(tc.tile_pool(name="reuse", bufs=1))

        scale_table = keep.tile([P, T], U8, name="scale_table", tag="shared", align_bytes=ALIGN)
        nc.gpsimd.memset(scale_table[:].bitcast(I32), 0)
        word_table = keep.tile([P, T], I32, name="word_table", align_bytes=ALIGN)
        words_in = x_words[0].rearrange("p n t -> p (n t)").bitcast(I32)
        nc.sync.dma_start(word_table[:, :HEAD], words_in[:, :HEAD])
        lists = []
        for t, src in enumerate((offs, tap1, tap2)):
            offsets = keep.tile([P, S // 16], U16, name=f"list{t}", align_bytes=ALIGN)
            nc.sync.dma_start(offsets[:], src)
            lists.append(offsets)
        nc.sync.dma_start(scale_table[TABLE_ROW:P:8, :].bitcast(I32), x_scales[0].bitcast(I32))
        warm = keep.tile([P, 16], F32, name="warm")
        nc.gpsimd.memset(warm[:, 0:1], 0.0)
        nc.scalar.activation(warm[:, 8:9], warm[:, 0:1], mybir.ActivationFunctionType.Sigmoid)
        x_plane = keep.tile([P, TAPS * S], U8, name="x_plane", align_bytes=ALIGN)
        nc.gpsimd.memset(x_plane[:].bitcast(I32), 0)

        weights = {"g": (w4, w5, w6), "o": (w1, w2, w3)}
        raw = {}

        def load(kind, t, piece, first, count):
            lo, hi = first * BLOCK, (first + count) * BLOCK
            nc.sync.dma_start(piece, weights[kind][t].rearrange("(p j) m -> p j m", j=PACK)[:, :, lo:hi])
            for b in range(count):
                raw[kind, t, first + b] = (piece, b * BLOCK)

        early = [reuse.tile([P, PACK, N], F32, name=f"early{u}", offset=RAW_BYTES * u, align_bytes=ALIGN) for u in range(2)]
        load("g", 0, early[0][:], 0, BLOCKS)
        nc.sync.dma_start(word_table[:, HEAD:], words_in[:, HEAD:])
        load("g", 1, early[1][:], 0, BLOCKS)

        picked_scales = keep.tile([P, TAPS * S], U8, name="picked_scales", align_bytes=ALIGN)
        for t in range(TAPS):
            nc.vector.tensor_copy(picked_scales[:, t * S : (t + 1) * S], scale_table[:].indirect(lists[t][:]))
        for i in range(4):
            nc.sync.dma_start(x_plane[i:P:32, :].bitcast(I32), picked_scales[8 * i + TABLE_ROW : P : 32, :].bitcast(I32))
        late = keep.tile([P, 15 * PACK * BLOCK], F32, name="late", tag="shared", align_bytes=ALIGN)
        at = 0
        spot = {}
        for kind, t, first, count, where in [("g", 2, 0, 4, None), ("o", 0, 0, 4, None), ("o", 1, 0, 4, None)] + [("o", 2, b, 1, 0 if b == 1 else None) for b in range(BLOCKS)]:
            size = PACK * count * BLOCK
            if where is None:
                load(kind, t, late[:, at : at + size].rearrange("p (j m) -> p j m", j=PACK), first, count)
                spot[kind, t, first] = at
                at = at + size
            else:
                piece = reuse.tile([P, PACK, count * BLOCK], F32, name=f"raw_{kind}{t}{first}", offset=where, align_bytes=ALIGN)
                load(kind, t, piece[:], first, count)

        picked = {}

        def pick(t, tag):
            picked[t] = keep.tile([P, S], U32, name=f"picked{t}", tag=tag, align_bytes=ALIGN)
            nc.vector.tensor_copy(picked[t][:], word_table[:].bitcast(U32).indirect(lists[t][:]))

        acc = {}
        for kind in ("g", "o"):
            for b in range(BLOCKS):
                acc[kind, b] = psum.tile([P, S], F32, name=f"acc_{kind}{b}")

        rounded = {}

        def place(shape, dtype, name, where):
            if where is None:
                return keep.tile(shape, dtype, name=name, align_bytes=ALIGN)
            return reuse.tile(shape, dtype, name=name, offset=where, align_bytes=ALIGN)

        def cast(engines, kind, t, first, count):
            stage = keep.tile([P, count * BLOCK, PACK], BF16, name=f"bf_{kind}{t}{first}", align_bytes=ALIGN)
            for b in range(count):
                rounded[kind, t, first + b] = (stage, b * BLOCK)
            piece, at = raw[kind, t, first]
            share = count * BLOCK // len(engines)
            for u, engine in enumerate(engines):
                dst = stage[:, u * share : (u + 1) * share, :].rearrange("p (c i) j -> p c j i", i=RUN)
                src = piece[:, :, at + u * share : at + (u + 1) * share].rearrange("p j (c i) -> p c j i", i=RUN)
                if engine == "s":
                    nc.scalar.copy(dst, src)
                else:
                    nc.vector.tensor_copy(dst, src)

        codes = {}
        passes = {}

        def quantise(kind, t, first, count, where=None):
            width = count * BLOCK
            words = keep.tile([P, width], U32, name=f"q_{kind}{t}{first}", align_bytes=ALIGN)
            plane = place([P, width], U8, f"s_{kind}{t}{first}", where)
            stage, at = rounded[kind, t, first]
            nc.vector.quantize_mx(out=words[:].bitcast(FP8X4), scales=plane[:], in_=stage[:, at : at + width, :].rearrange("p c j -> p (c j)"))
            for b in range(count):
                cols = slice(b * BLOCK, (b + 1) * BLOCK)
                codes[kind, t, first + b] = (words[:, cols], plane[:, cols])

        def matmul(kind, t, b):
            words, plane = codes[kind, t, b]
            seen = passes.get((kind, b), 0)
            passes[kind, b] = seen + 1
            nc.tensor.matmul_mx(out=acc[kind, b][:], lhsT=words.bitcast(FP8X4), lhsT_scale=plane,
                                rhs=picked[t][:].bitcast(FP8X4), rhs_scale=x_plane[:, t * S : (t + 1) * S],
                                start=(seen == 0), stop=(seen == TAPS - 1))

        def multiply(kind, t, first, count, where=None):
            quantise(kind, t, first, count, where)
            for b in range(first, first + count):
                matmul(kind, t, b)

        gate = {}

        def sigmoid(b, where=None):
            gate[b] = place([P, S], F32, f"gate{b}", where)
            nc.scalar.activation(gate[b][:], acc["g", b][:], mybir.ActivationFunctionType.Sigmoid)

        def finish(b, lo=0, hi=S, over=None):
            if over is None:
                res = keep.tile([P, hi - lo], F32, name=f"res{b}_{lo}", align_bytes=ALIGN)[:]
            else:
                res = late[:, over : over + hi - lo]
            nc.vector.tensor_tensor(res, acc["o", b][:, lo:hi], gate[b][:, lo:hi], mybir.AluOpType.mult)
            nc.sync.dma_start(out[b * BLOCK : (b + 1) * BLOCK, lo:hi], res)

        pick(0, "picked0")
        for first in (0, 2):
            cast("s", "g", 0, first, 2)
            multiply("g", 0, first, 2)
        pick(1, "bf_g02")
        pick(2, "picked2")
        cast("s", "g", 1, 0, 2)
        multiply("g", 1, 0, 2)
        cast("s", "g", 1, 2, 2)
        quantise("g", 1, 2, 2)
        for b in range(BLOCKS):
            cast("v" if b < 2 else "s", "g", 2, b, 1)
        for b in range(BLOCKS):
            multiply("g", 2, b, 1)
            if b >= 2:
                matmul("g", 1, b)
        for b in range(BLOCKS):
            sigmoid(b)
        for first in (0, 2):
            cast("v", "o", 0, first, 2)
        for first in (0, 2):
            multiply("o", 0, first, 2)
        cast("v", "o", 1, 0, 2)
        cast("s", "o", 1, 2, 2)
        for b in range(BLOCKS):
            cast("v" if b < 1 else "s", "o", 2, b, 1)
        multiply("o", 1, 0, 1)
        multiply("o", 2, 0, 1)
        multiply("o", 1, 1, 1)
        multiply("o", 1, 2, 1)
        multiply("o", 2, 1, 1)
        multiply("o", 1, 3, 1, 0)
        finish(0)
        multiply("o", 2, 2, 1)
        finish(1)
        multiply("o", 2, 3, 1)
        finish(2)
        finish(3, 0, HALF)
        finish(3, HALF, S)
